import numpy as np, ml_dtypes
CORES = [0,1,2,3]
N = 4
PERM = [[0,3],[3,0],[1,2],[2,1]]
def setup_inputs(rng):
    return {"x": rng.standard_normal((N, 128, 64), dtype=np.float32).astype(ml_dtypes.bfloat16)}
def reference(x):
    y = np.empty_like(x)
    for s, d in PERM:
        y[d] = x[s]
    return {"y": y}

SCRATCH = {
    "send": ("dram", [128, 64], "bfloat16"),
    "land": ("dram", [128, 64], "bfloat16"),
}
SEMAPHORES = ["loaded", "sent", "arrived", "stored"]


def rank_program(g, core, T, topo):
    rank = T.rank_of(core)
    if rank is None:
        return
    perm = T.tables["PERM"]
    dsts = [d for s, d in perm if s == rank]
    srcs = [s for s, d in perm if d == rank]
    sem = T.sem

    sends = bool(dsts) and dsts[0] != rank
    takes = bool(srcs) and srcs[0] != rank

    if sends:
        g.sync.dma_start(T.send[:], T.x[:]).then_inc(sem.loaded, 16)

    if sends:
        dst_core = T.cores[dsts[0]]
        rid, pid, _se = topo.addr(dst_core)
        g.wait_ge(sem.loaded, 16)
        g.remote_dma(T.land[:], T.send[:], remote_sem=sem.arrived, local_sem=sem.sent,
                     pid=pid, routing_id=rid, dma_engine_mask=topo.mask(core, dst_core))

    if takes:
        g.sync.wait_ge(sem.arrived, 16)
        g.sync.dma_start(T.y[:], T.land[:]).then_inc(sem.stored, 16)
    elif srcs:
        g.sync.dma_start(T.y[:], T.x[:]).then_inc(sem.stored, 16)

    if sends:
        g.wait_ge(sem.sent, 16)
    if srcs:
        g.wait_ge(sem.stored, 16)
